import numpy as np, ml_dtypes
CORES = [5,29,101,125,133,157,229,253]
N = 8
BF = ml_dtypes.bfloat16
def gentries(a):
    return np.ascontiguousarray(a.reshape(8, 16, -1).transpose(0, 2, 1)).reshape(8, -1)
def gtable(e):
    e = np.asarray(e); return np.ascontiguousarray(e.reshape(8, -1, 16).transpose(0, 2, 1)).reshape(128, -1).astype(np.int32)
W, V, KC, R = 2816, 2048, 32, 3
LO, HI = 20, 175
def peps(rng):
    p = rng.integers(LO, HI + 1, (N, 8, V, 16)); i = np.arange(16); s = rng.integers(0, 15, (N, 8, V // 2, 1))
    p[:, :, 1::2] = np.take_along_axis(p[:, :, 0::2], np.where(i == s, s + 1, np.where(i == s + 1, s, i)), axis=-1); return p
def wants(rng):
    w = rng.integers(0, V, (N, 8, N, KC)); w[..., 1::2] = np.where(rng.random((N, 8, N, KC // 2)) < 0.25, w[..., 0::2] ^ 1, w[..., 1::2])
    w[..., KC - 1] = w[..., 2]; return w
def own(rng):
    e = np.argsort(rng.random((N, 8, V // 2)), axis=-1)[:, :, :N * KC // 2]; x = rng.integers(0, 2, e.shape)
    return np.stack([2 * e + x, 2 * e + 1 - x], axis=-1).reshape(N, 8, N, KC).transpose(2, 1, 0, 3).copy()
def bins(p, w):
    m = p[np.arange(N)[None, None, :, None], np.arange(8)[None, :, None, None], w].reshape(N, 8, N * KC, 16)
    b = np.add.accumulate(m, axis=-1); return b, b[..., -1:] + 64 - b
def noise(rng):
    return rng.integers(1, 4, (N, 8, 16, W)) * (rng.random((N, 8, 16, W)) < 0.3)
def some(rng):
    return np.argsort(rng.random((N, 8, N * KC)), axis=-1)[..., :R + 1]
def shine(rng, s, b, y, n, a, z):
    for r in range(N):
        for g in range(8):
            for t in n[r, g]:
                s[r, g][:, b[r, g, t]] = rng.integers(a, z + 1, (16, 16)); s[r, g][:, y[r, g, t]] = rng.integers(a, z + 1, (16, 16))
def pack(s, p, w):
    return {"spec": s.reshape(N, 128, W).astype(np.float32).astype(BF), "pep": p.transpose(0, 1, 3, 2).reshape(N, 128, V).astype(np.float32).astype(BF),
            "want": np.stack([gtable(w[r].reshape(8, N * KC)) for r in range(N)])}
def setup_inputs(rng):
    p, w, s, n = peps(rng), wants(rng), noise(rng), some(rng); b, y = bins(p, w)
    n[:, ::2, 0] = KC * rng.integers(0, N, (N, 4)) + 2; shine(rng, s, b, y, n, 4, 15)
    return pack(s, p, w)
def setup_inputs_kin(rng):
    p, w, s = peps(rng), own(rng), noise(rng); b, y = bins(p, w)
    n = 2 * np.argsort(rng.random((N, 8, N * KC // 2)), axis=-1)[..., :R + 1]
    shine(rng, s, b, y, n[..., 1:], 5, 9); shine(rng, s, b, y, n[..., :1], 12, 15)
    return pack(s, p, w)
def setup_inputs_twins(rng):
    p, w, s, n = peps(rng), own(rng), noise(rng), np.zeros((N, 8, 1), np.int64)
    for r in range(N):
        for g in range(8):
            q, k = [int(v) for v in rng.permutation(N)[:2]]; i, j = sorted([KC * q + int(rng.integers(KC)), KC * k + int(rng.integers(KC))])
            if g == 0: i, j = 0, N * KC - 1
            if g == 1: i = KC * q + int(rng.integers(KC - 1)); j = i + 1; w[r, g, q, j % KC] = w[r, g, q, i % KC]
            if g == 2: i, j = KC - 1, KC
            p[j // KC, g, w[r, g, j // KC, j % KC]] = p[i // KC, g, w[r, g, i // KC, i % KC]]; n[r, g, 0] = i
    b, y = bins(p, w); shine(rng, s, b, y, some(rng), 5, 9); shine(rng, s, b, y, n, 15, 15)
    s[:, 3] = rng.integers(1, 16, (N, 16, 1)); return pack(s, p, w)
def setup_inputs_ends(rng):
    p, w, s, n = peps(rng), wants(rng), noise(rng), np.zeros((N, 8, 1), np.int64)
    p[0, :, 0] = LO; p[N - 1, :, V - 1] = HI; p[:, :, 1] = 64; p[:, :, 2] = HI; p[:, :, 2, 0] = LO
    w[..., 0] = 0; w[..., 1] = 1; w[..., 2] = 2; w[..., KC - 1] = V - 1
    n[:, 0::4] = 1; n[:, 1::4] = 0; n[:, 2::4] = N * KC - 1; n[:, 3::4] = 2
    b, y = bins(p, w); shine(rng, s, b, y, some(rng), 5, 9); shine(rng, s, b, y, n, 15, 15)
    s[..., 0] = 15; s[..., W - 1] = 15; return pack(s, p, w)
def setup_inputs_dark(rng):
    p, w, s = peps(rng), own(rng), noise(rng)
    for r in range(N):
        for g in range(8): p[0, g, w[r, g, 0, 0], 0] = LO
    b, y = bins(p, w); shine(rng, s, b, y, some(rng), 4, 15)
    for r in range(N):
        d = rng.permutation(8)
        for g in d[:3]: s[r, g][:, y[r, g].reshape(-1)] = 0; s[r, g][:, LO] = rng.integers(1, 16, 16)
        s[r, d[3]] = 0
        g = d[4]; t = int(rng.integers(1, N * KC)); s[r, g][:, y[r, g].reshape(-1)] = 0
        s[r, g][:, b[r, g, t]] = rng.integers(8, 16, (16, 16)); s[r, g][:, y[r, g, t]] = rng.integers(8, 16, (16, 16))
    return pack(s, p, w)
def setup_inputs_spread(rng):
    p = np.minimum(HI, LO + ((HI - LO + 1) * rng.random((N, 8, V, 16)) ** 3).astype(np.int64)); k = (N, 8, 1, W)
    s = (rng.integers(0, 16, (N, 8, 16, W)) >> rng.integers(0, 3, k)) * (rng.random(k) > 0.0625)
    return pack(s, p, wants(rng))
def check_inputs(d):
    bad = []; s = d["spec"].astype(np.float32); p = d["pep"].astype(np.float32); w = d["want"]
    if not ((s >= 0) & (s <= 15) & (s == np.floor(s))).all(): bad.append("spec")
    if not ((p >= LO) & (p <= HI) & (p == np.floor(p))).all(): bad.append("pep")
    if not ((w >= 0) & (w < V)).all(): bad.append("want")
    return bad
def reference(spec, pep, want):
    left = spec.astype(np.float32).reshape(N, 8, 16, W); m_ = pep.astype(np.float32).astype(np.int64).reshape(N, 8, 16, V)
    win = np.zeros((N, 8, R), np.float32); score = np.zeros((N, 8, R), np.float32)
    for r in range(N):
        e = gentries(want[r]).reshape(8, N, KC)
        for g in range(8):
            m = np.concatenate([m_[q, g][:, e[g, q]] for q in range(N)], axis=1)
            b = np.add.accumulate(m, axis=0); y = b[15] + 64 - b
            s = left[r, g]
            for t in range(R):
                sc = np.sum(s[:, b] * s[:, y], axis=(0, 1))
                n = int(np.argmax(sc)); win[r, g, t] = n; score[r, g, t] = sc[n]
                s[:, b[:, n]] = 0; s[:, y[:, n]] = 0
    return {"win": win, "score": score, "left": left.reshape(N, 128, W).astype(BF)}

from concourse.bass import DstId, RemoteDMATransfer
from concourse.mybir import AluOpType as A, AxisListType as X, ActivationFunctionType as F

W, V, KC, NR = 2816, 2048, 32, 8
NC = KC * NR
PAIRS = 6
BIAS = 28800
FAR_CHUNKS = [22, 22, 20, 22, 22, 20]

SCRATCH = {
    "wd": ("dram", [128, 16], "int32"),
    "wland": ("sbuf", [128, NR, 16], "int32"),
    "roff": ("sbuf", [128, 16], "uint16"),
    "peps": ("sbuf", [128, V], "bfloat16"),
    "sp": ("sbuf", [128, W], "bfloat16"),
    "resp": ("sbuf", [128, NC], "bfloat16"),
    "ms": ("sbuf", [128, NC], "bfloat16"),
    "rl": ("sbuf", [128, 2 * KC], "bfloat16"),
    "offb": ("sbuf", [128, NC], "uint16"),
    "offy": ("sbuf", [128, NC], "uint16"),
    "gb": ("sbuf", [128, 16 * NC], "bfloat16"),
    "pr": ("sbuf", [128, 16 * NC], "bfloat16"),
    "jj": ("sbuf", [128, 144], "float32"),
    "jg": ("sbuf", [128, 128], "float32"),
    "pi": ("sbuf", [128, 2], "int32"),
    "cols": ("sbuf", [128, 4], "float32"),
    "lb": ("sbuf", [128, 128], "bfloat16"),
    "ly": ("sbuf", [128, 128], "bfloat16"),
    "ge": ("sbuf", [128, 128], "bfloat16"),
    "bo": ("sbuf", [128, 128], "bfloat16"),
    "bok": ("sbuf", [128, 128], "bfloat16"),
    "bok32": ("sbuf", [128, 128], "float32"),
    "id32": ("sbuf", [128, 128], "float32"),
    "negi": ("sbuf", [128, 128], "bfloat16"),
    "wm": ("sbuf", [128, 144], "bfloat16"),
    "coef": ("sbuf", [128, 32], "bfloat16"),
    "tmpc": ("sbuf", [128, 16], "bfloat16"),
    "cc": ("sbuf", [128, 32], "bfloat16"),
    "kt": ("sbuf", [128, NC], "bfloat16"),
    "ones": ("sbuf", [128, 128], "bfloat16"),
    "zeros": ("sbuf", [128, NC], "bfloat16"),
    "cq": ("sbuf", [128, 4], "float32"),
    "bins": ("sbuf", [128, 2 * NC], "float32"),
    "key": ("sbuf", [128, 4], "float32"),
    "qq": ("sbuf", [128, 12], "int32"),
    "woff": ("sbuf", [128, 12], "uint16"),
    "zoff": ("sbuf", [128, 96], "uint16"),
    "mw": ("sbuf", [128, 64], "bfloat16"),
    "sc": ("sbuf", [128, 64], "float32"),
    "mid": ("sbuf", [128, 16], "float32"),
    "hi": ("sbuf", [128, 16], "float32"),
    "lo": ("sbuf", [128, 16], "float32"),
    "rad": ("sbuf", [128, 16], "bfloat16"),
    "uu": ("sbuf", [128, 2 * NC], "float32"),
    "u16": ("sbuf", [128, 2 * NC], "uint16"),
    "vv": ("sbuf", [128, PAIRS * 2 * NC], "bfloat16"),
    "eq": ("sbuf", [128, (16 - PAIRS) * 2 * NC], "bfloat16"),
    "pm": ("sbuf", [128, NC], "float32"),
    "res": ("sbuf", [128, 8], "float32"),
    "pb": ("psum", [128, 512], "float32"),
    "py": ("psum", [128, 512], "float32"),
    "pt": ("psum", [128, 512], "float32"),
    "acc": ("psum", [128, 512], "float32"),
    "pk0": ("psum", [128, 512], "float32"),
    "pk1": ("psum", [128, 512], "float32"),
    "pc0": ("psum", [128, 512], "float32"),
    "pc1": ("psum", [128, 512], "float32"),
}
SEMAPHORES = ["cv", "cs", "cp", "cg", "ldd", "ldw", "ldp", "lds", "go", "sent", "reqr", "reqd", "reqx",
              "rspr", "rspd", "rspx", "stl", "sto"]


def bits(engs):
    m = 0
    for e in engs:
        m |= 1 << e
    return m


def layout(T, topo, r):
    me = T.cores[r]
    near = [q for q in range(NR) if q != r and topo.may_write(me, T.cores[q])]
    far = [q for q in range(NR) if q != r and q not in near]
    helpers = [c for c in topo.cores_of(me) if T.rank_of(c) is None and all(topo.may_write(c, T.cores[q]) for q in far)]
    helpers.sort(key=lambda c: (topo.die(c) != topo.die(me), c))
    return near, far, helpers


def slots(T, topo, r):
    near, far, _ = layout(T, topo, r)
    return [r] + near + far


def shares(engs, n):
    size = [1] * n
    k = 0
    while sum(size) + size[k % n] <= len(engs):
        size[k % n] *= 2
        k += 1
    out, a = [], 0
    for s in size:
        out.append(engs[a:a + s])
        a += s
    return out


def inner_engines(T, topo, r):
    near, far, helpers = layout(T, topo, r)
    me = T.cores[r]
    outer = topo.engines(me, T.cores[near[0]])
    return [e for e in topo.engines(me, helpers[0]) if e not in outer]


def dst(topo, to, frm):
    rid, pid = topo.addr(to, frm)
    return DstId(rid=rid, pnc=pid)


def helper_program(g, core, T, topo):
    owner = [r for r in range(NR) if core in topo.cores_of(T.cores[r])]
    if not owner:
        return
    r = owner[0]
    near, far, helpers = layout(T, topo, r)
    if core not in helpers[:len(far)]:
        return
    j = helpers.index(core)
    inner = inner_engines(T, topo, r)
    S = T.sem
    q = far[j]
    g.wait_ge(S.reqr, len(shares(inner, len(far))[j]))
    engs = topo.engines(core, T.cores[q])
    rid, pid = topo.addr(T.cores[q], core)
    g.remote_dma(T.wland[:, slots(T, topo, q).index(r), :], T.wd[:], S.reqx, S.sent, pid, rid, bits(engs))
    sent = len(engs)
    if j < 2:
        g.wait_ge(S.rspr, len(shares(inner, 2)[j]))
        tr = []
        for h, sh in enumerate(shares(engs, 2)):
            tr.append(RemoteDMATransfer(dst_ids=[dst(topo, T.cores[far[2 * j + h]], core)], dma_engine_mask=bits(sh),
                                        remote_sem=S.rspx, src=T.rl[:, KC * h:KC * h + KC], dst=T.ms[:, KC * r:KC * r + KC]))
            sent += len(sh)
        g.remote_dma_fused(tr, local_sem=S.sent)
    g.wait_ge(S.sent, sent)


def rank_program(g, core, T, topo):
    r = T.rank_of(core)
    if r is None:
        helper_program(g, core, T, topo)
        return
    S = T.sem
    near, far, helpers = layout(T, topo, r)
    order = [r] + near + far
    nn, nf = len(near), len(far)
    inner = inner_engines(T, topo, r)
    outer = topo.engines(core, T.cores[near[0]])
    Q = {"v": g.vector, "s": g.scalar, "p": g.tensor, "g": g, "y": g.sync}
    cnt = {"v": 0, "s": 0, "p": 0, "g": 0}
    waited = {k: {} for k in Q}
    writer, readers, bank = {}, {}, {}

    def wait(q, tok):
        if waited[q].get(tok[0], 0) < tok[1]:
            waited[q][tok[0]] = tok[1]
            Q[q].wait_ge(S[tok[0]], tok[1])

    def before(q, rd, wr, banks=()):
        need = {}
        toks = [writer[k] for k in rd if k in writer]
        for k in wr:
            toks += readers.get(k, [])
            if k in writer and not (q == "p" and writer[k][0] == "cp"):
                toks.append(writer[k])
        for b in banks:
            toks += [t for e, t in bank.get(b, {}).items() if e != q]
        for s, n in toks:
            need[s] = max(need.get(s, 0), n)
        for s, n in need.items():
            wait(q, (s, n))

    def op(q, call, rd=(), wr=(), banks=()):
        before(q, rd, wr, banks)
        cnt[q] += 1
        tok = ("c" + q, cnt[q])
        call().then_inc(S[tok[0]], 1)
        for k in rd:
            readers.setdefault(k, []).append(tok)
        for k in wr:
            writer[k] = tok
            readers[k] = []
        for b in banks:
            bank.setdefault(b, {})[q] = tok
        return tok

    vec, act, pe = g.vector, g.scalar, g.tensor

    def ts(out, in0, s1, s2, o0, o1, rd, wr, banks=()):
        if o1 is None:
            return op("v", lambda: vec.tensor_scalar(out, in0, s1, None, o0), rd, wr, banks)
        return op("v", lambda: vec.tensor_scalar(out, in0, s1, s2, o0, o1), rd, wr, banks)

    def tt(out, a, b, o, rd, wr):
        return op("v", lambda: vec.tensor_tensor(out, a, b, o), rd, wr)

    def cp(out, a, rd, wr, banks=()):
        return op("v", lambda: vec.tensor_copy(out, a), rd, wr, banks)

    def fill(ap, c, wr):
        return op("v", lambda: vec.memset(ap, c), (), wr)

    def mm(b, out, lhs, rhs, start, stop, rd, wr):
        return op("p", lambda: pe.matmul(out, lhs, rhs, start, stop), rd, wr, [b])

    g.sync.dma_start(T.wd[:], T.want[:]).then_inc(S.ldd, 16)
    act.dma_start(T.wland[:, 0, :], T.want[:]).then_inc(S.ldw, 16)
    g.sync.dma_start(T.peps[:], T.pep[:]).then_inc(S.ldp, 16)
    writer["wd"], writer["w0"], writer["peps"], writer["sp"] = ("ldd", 16), ("ldw", 16), ("ldp", 16), ("lds", 16)
    writer["w1"] = ("reqd", len(outer) * nn)
    writer["w2"] = ("reqx", sum(len(topo.engines(layout(T, topo, q)[2][layout(T, topo, q)[1].index(r)], core)) for q in far))
    writer["m1"] = ("rspd", sum(len(shares(outer, nn)[layout(T, topo, q)[0].index(r)]) for q in near))
    writer["m2"] = ("rspx", nf * len(shares(outer, 2)[0]))

    op("g", lambda: g.iota(T.pi[:, 0:1], [[1, 1]], 0, 1), (), ["pi0"])
    op("g", lambda: g.iota(T.jj[:], [[1, 144]], 0, 0, allow_small_or_imprecise_dtypes=True), (), ["jj"])
    op("g", lambda: g.iota(T.jg[:], [[16, 8], [0, 16]], 0, 0, allow_small_or_imprecise_dtypes=True), (), ["jg"])
    fill(T.kt[0:2, :], 256.0 * BIAS, ["kt"])
    fill(T.ones[0:2, :], 1.0, ["ones"])
    fill(T.zeros[:], 0.0, ["zeros"])
    fill(T.cq[:, 0:3], -127.5, ["cq0"])
    fill(T.cq[:, 3:4], -127.5 - NC, ["cq1"])
    fill(T.cc[:, 0:16], -4.0, ["cc0"])
    fill(T.cc[:, 16:17], 4.0, ["cc1"])
    fill(T.cc[:, 17:18], -4.0, ["cc2"])
    fill(T.coef[:, 16:32], 1.0, ["coef1"])
    pf, icol, gcol = T.cols[:, 0:1], T.cols[:, 1:2], T.cols[:, 2:3]
    ts(T.pi[:, 1:2], T.pi[:, 0:1], 15, None, A.bitwise_and, None, ["pi0"], ["pi1"])
    cp(pf, T.pi[:, 0:1], ["pi0"], ["pf"])
    cp(icol, T.pi[:, 1:2], ["pi1"], ["icol"])
    ts(T.ge[:], T.jj[:, 0:128], pf, None, A.is_ge, None, ["jj", "pf"], ["ge"])
    ts(gcol, pf, icol, None, A.subtract, None, ["pf", "icol"], ["gcol"])
    ts(T.negi[:], T.jj[:, 0:128], pf, -4096.0, A.is_equal, A.mult, ["jj", "pf"], ["negi"])
    ts(T.bo[:], T.jg[:], gcol, None, A.is_equal, None, ["jg", "gcol"], ["bo"])
    ts(T.wm[:], T.jj[:], gcol, 15.0, A.subtract, A.is_equal, ["jj", "gcol"], ["wm"])
    tt(T.lb[:], T.bo[:], T.ge[:], A.mult, ["bo", "ge"], ["lb"])
    ts(T.bok[:], T.jg[:], gcol, -256.0, A.is_equal, A.mult, ["jg", "gcol"], ["bok"])
    tt(T.ly[:], T.bo[:], T.lb[:], A.subtract, ["bo", "lb"], ["ly"])
    ts(T.tmpc[:], T.jj[:, 0:16], icol, 2.0, A.is_ge, A.mult, ["jj", "icol"], ["tmpc"])
    ts(T.bok32[:], T.jg[:], gcol, -256.0, A.is_equal, A.mult, ["jg", "gcol"], ["bok32"])
    ts(T.coef[:, 0:16], T.tmpc[:], -1.0, None, A.add, None, ["tmpc"], ["coef0"])
    ts(T.id32[:], T.jj[:, 0:128], pf, None, A.is_equal, None, ["jj", "pf"], ["id32"])

    before("g", ["wd"], [])
    tr = [RemoteDMATransfer(dst_ids=[dst(topo, helpers[j], core)], dma_engine_mask=bits(sh), remote_sem=S.reqr,
                            src=T.wd[:], dst=T.wd[:]) for j, sh in enumerate(shares(inner, nf))]
    g.remote_dma_fused(tr, local_sem=S.sent)
    sent = sum(len(sh) for sh in shares(inner, nf))
    g.remote_dma_fused([RemoteDMATransfer(dst_ids=[dst(topo, T.cores[q], core) for q in near], dma_engine_mask=bits(outer),
                                          remote_sem=S.reqd, srcs=[T.wd[:]],
                                          dsts=[T.wland[:, slots(T, topo, q).index(r), :] for q in near])], local_sem=S.sent)
    sent += len(outer)
    g.sem_inc(S.go, 1)
    g.sync.wait_ge(S.go, 1)
    g.sync.dma_start(T.sp[:], T.spec[:]).then_inc(S.lds, 16)

    a, parts = 0, []
    before("g", [], ["kt"])
    while a < NR:
        b = a + 1
        step = order[b] - order[a] if b < NR else 0
        while b < NR and order[b] - order[b - 1] == step:
            b += 1
        op("g", lambda: g.iota(T.kt[0:1, KC * a:KC * b], [[KC * step, b - a], [1, KC]], KC * order[a], 0,
                               allow_small_or_imprecise_dtypes=True), (), ["kt%d" % a])
        parts.append("kt%d" % a)
        a = b

    PK = [("pk0", T.pk0), ("pk1", T.pk1), ("pk0", T.pk0)]
    PC = [("pc0", T.pc0), ("pc1", T.pc1)]

    def open_key(t):
        n, p = PK[t]
        return mm(n, p[:, 0:NC], T.ones[0:2, :], T.kt[0:2, :], True, False, ["ones", "kt"] + parts, [n])

    mm("acc", T.acc[:, 0:NC], T.bo[:], T.zeros[:], True, False, ["bo", "zeros"], ["acc"])
    for n, p in PC:
        mm(n, p[:, 0:18], T.bo[:], T.cc[:, 0:18], True, False, ["bo", "cc0", "cc1", "cc2"], [n])
    open_key(0)
    opened = open_key(1)

    def serve(k, a, b, out, name):
        cp(T.roff[:, 2 * a:2 * b], T.wland[:, a:b, 2 * r:2 * r + 2], ["w%d" % k], ["roff%d" % k])
        cp(out, T.peps[:, 0:V].indirect(T.roff[:, 2 * a:2 * b]), ["roff%d" % k, "peps"], [name])

    serve(0, 0, 1, T.ms[:, KC * r:KC * r + KC], "m0")
    serve(1, 1, 1 + nn, T.resp[:, KC:KC * (1 + nn)], "resp1")
    before("g", ["resp1"], [])
    tr = [RemoteDMATransfer(dst_ids=[dst(topo, T.cores[near[j]], core)], dma_engine_mask=bits(sh), remote_sem=S.rspd,
                            src=T.resp[:, KC * (1 + j):KC * (2 + j)], dst=T.ms[:, KC * r:KC * r + KC])
          for j, sh in enumerate(shares(outer, nn))]
    g.remote_dma_fused(tr, local_sem=S.sent)
    sent += sum(len(sh) for sh in shares(outer, nn))
    serve(2, 1 + nn, NR, T.resp[:, KC * (1 + nn):NC], "resp2")
    before("g", ["resp2"], [])
    tr = [RemoteDMATransfer(dst_ids=[dst(topo, helpers[j], core)], dma_engine_mask=bits(sh), remote_sem=S.rspr,
                            src=T.resp[:, KC * (1 + nn + 2 * j):KC * (3 + nn + 2 * j)], dst=T.rl[:])
          for j, sh in enumerate(shares(inner, 2))]
    g.remote_dma_fused(tr, local_sem=S.sent)
    sent += sum(len(sh) for sh in shares(inner, 2))

    def bins(k, a, b):
        for n, p, tri, name in (("pb", T.pb, T.lb, "lb"), ("py", T.py, T.ly, "ly")):
            for s in range(a, b):
                mm(n, p[:, KC * s:KC * s + KC], tri[:], T.ms[:, KC * order[s]:KC * order[s] + KC], True, True,
                   [name, "m%d" % k], ["%s%d" % (n, k)])

    def offsets(k, a, b):
        cp(T.offb[:, KC * a:KC * b], T.pb[:, KC * a:KC * b], ["pb%d" % k], ["offb%d" % k], ["pb"])
        ts(T.offy[:, KC * a:KC * b], T.py[:, KC * a:KC * b], 64.0, None, A.add, None, ["py%d" % k], ["offy%d" % k], ["py"])

    done = []

    def products(k, c0, c1):
        lo, hi = 16 * c0, 16 * c1
        op("s", lambda: act.activation(T.gb[:, lo:hi], T.sp[:, 0:W].indirect(T.offb[:, c0:c1]), F.Copy),
           ["sp", "offb%d" % k], ["gb%d" % c0])
        tt(T.pr[:, lo:hi], T.sp[:, 0:W].indirect(T.offy[:, c0:c1]), T.gb[:, lo:hi], A.mult,
           ["sp", "offy%d" % k, "gb%d" % c0], ["pr%d" % c0])
        done.append((c0, c1))

    def sums(c0, c1, last):
        rd = ["pr%d" % a for a, b in done if a < c1 and b > c0]
        for i in range(16):
            mm("pk0", T.pk0[:, c0:c1], T.bok[:], T.pr[:, 16 * c0 + i:16 * c1:16], False, last and i == 15, rd + ["bok"], ["pk0"])
        for i in range(16):
            mm("acc", T.acc[:, c0:c1], T.wm[:, 15 - i:143 - i], T.pr[:, 16 * c0 + i:16 * c1:16], False, False, rd + ["wm"], ["acc"])

    wait("p", opened)
    bins(0, 0, 1)
    offsets(0, 0, 1)
    products(0, 0, KC)
    bins(1, 1, 1 + nn)
    offsets(1, 1, 1 + nn)
    for s in range(1, 1 + nn):
        products(1, KC * s, KC * s + KC)
    half = KC * (1 + nn)
    sums(0, half // 2, False)
    bins(2, 1 + nn, NR)
    offsets(2, 1 + nn, NR)
    mm("pt", T.pt[:, 0:NC], T.lb[:], T.ms[:], True, True, ["lb", "m0", "m1", "m2"], ["pt0"])
    mm("pt", T.pt[:, NC:2 * NC], T.ly[:], T.ms[:], True, True, ["ly", "m0", "m1", "m2"], ["pt1"])
    sums(half // 2, half, False)
    c = half
    for n in FAR_CHUNKS:
        products(2, c, c + n)
        c += n
    third = (half + NC) // 2
    sums(half, third, False)
    sums(third, NC, True)
    op("s", lambda: act.activation(T.bins[:, 0:NC], T.pt[:, 0:NC], F.Copy), ["pt0"], ["bins0"], ["pt"])
    op("s", lambda: act.activation(T.bins[:, NC:2 * NC], T.pt[:, NC:2 * NC], F.Identity, bias=64.0), ["pt1"], ["bins1"], ["pt"])

    def pick(t):
        z = 32 * t
        cp(T.zoff[:, z:z + 32], T.bins[:, 0:2 * NC].indirect(T.woff[:, 4 * t + 2:4 * t + 4]), ["bins0", "bins1", "woff%d" % t], ["zoff%d" % t])

    def strike(t, h):
        z = 32 * t + 16 * h
        cp(T.sp[:, 0:W].indirect(T.zoff[:, z:z + 1]), T.zeros[:, 0:16], ["zoff%d" % t, "zeros"], ["sp"])

    def report(t):
        q0, k = T.qq[:, 4 * t:4 * t + 1], T.key[:, t:t + 1]
        ts(T.res[:, t:t + 1], q0, -256.0, k, A.mult, A.add, ["qq%d" % t, "key%d" % t], ["win%d" % t])
        ts(T.res[:, 4 + t:5 + t], q0, -1.0, float(BIAS), A.mult, A.add, ["qq%d" % t], ["score%d" % t])

    for t in range(3):
        n, p = PK[t]
        k = T.key[:, t:t + 1]
        op("v", lambda: vec.tensor_reduce(k, p[:, 0:NC], X.X, A.min), [n], ["key%d" % t], [n])
        ts(T.qq[:, 4 * t:4 * t + 4], T.cq[:], k, 1.0 / 256, A.add, A.mult, ["cq0", "cq1", "key%d" % t], ["qq%d" % t])
        ts(T.woff[:, 4 * t:4 * t + 4], T.qq[:, 4 * t:4 * t + 4], -256.0, k, A.mult, A.add, ["qq%d" % t, "key%d" % t], ["woff%d" % t])
        if t == 2:
            break
        z = 32 * t
        tt(T.mw[:, z:z + 32], T.ms[:, 0:NC].indirect(T.woff[:, 4 * t:4 * t + 2]), T.coef[:], A.mult,
           ["m0", "m1", "m2", "woff%d" % t, "coef0", "coef1"], ["mw%d" % t])
        cn, cpz = PC[t]
        mm(cn, cpz[:, 0:18], T.bo[:], T.mw[:, z:z + 18], False, True, ["bo", "mw%d" % t], [cn])
        if t == 0:
            open_key(2)
        sc = "sc%d" % t
        op("s", lambda: act.activation(T.sc[:, z:z + 18], cpz[:, 0:18], F.Abs), [cn], [sc], [cn])
        op("s", lambda: act.activation(T.uu[:, 0:NC], T.pb[:, 0:NC], F.Abs, bias=T.sc[:, z + 16:z + 17], scale=-2.0),
           [sc, "pb0", "pb1", "pb2"], ["u0"], ["pb"])
        op("s", lambda: act.activation(T.uu[:, NC:2 * NC], T.py[:, 0:NC], F.Abs, bias=T.sc[:, z + 17:z + 18], scale=-2.0),
           [sc, "py0", "py1", "py2"], ["u1"], ["py"])
        pick(t)
        strike(t, 0)
        ua, ub = T.sc[:, z:z + 2 * PAIRS:2], T.sc[:, z + 1:z + 2 * PAIRS:2]
        m0 = 8 * t
        tt(T.mid[:, m0:m0 + PAIRS], ua, ub, A.add, [sc], ["mid%d" % t])
        tt(T.hi[:, m0:m0 + PAIRS], ua, ub, A.max, [sc], ["hi%d" % t])
        tt(T.lo[:, m0:m0 + PAIRS], ua, ub, A.min, [sc], ["lo%d" % t])
        cp(T.u16[:, 0:NC], T.uu[:, 0:NC], ["u0"], ["u160"])
        tt(T.rad[:, m0:m0 + PAIRS], T.hi[:, m0:m0 + PAIRS], T.lo[:, m0:m0 + PAIRS], A.subtract, ["hi%d" % t, "lo%d" % t], ["rad%d" % t])
        cp(T.u16[:, NC:2 * NC], T.uu[:, NC:2 * NC], ["u1"], ["u161"])
        for j in range(PAIRS):
            op("s", lambda: act.activation(T.vv[:, 512 * j:512 * j + 512], T.uu[:], F.Abs, bias=T.mid[:, m0 + j:m0 + j + 1], scale=-2.0),
               ["u0", "u1", "mid%d" % t], ["vv%d" % j])
        tiles = 16 - PAIRS
        for j in range(tiles):
            e = T.eq[:, 512 * j:512 * j + 512]
            s = 16 - 2 * PAIRS
            if j < s:
                ts(e, T.u16[:], T.sc[:, z + 2 * PAIRS + j:z + 2 * PAIRS + j + 1], None, A.is_equal, None, ["u160", "u161", sc], ["eq%d" % j])
            else:
                i = j - s
                ts(e, T.vv[:, 512 * i:512 * i + 512], T.rad[:, m0 + i:m0 + i + 1], None, A.is_equal, None, ["vv%d" % i, "rad%d" % t], ["eq%d" % j])
            for h in (0, 1):
                mm("acc", T.acc[:, 0:NC], T.negi[:], T.eq[:, 512 * j + NC * h:512 * j + NC * h + NC], False,
                   j == tiles - 1 and h == 1, ["negi", "eq%d" % j], ["acc"])
        ts(T.pm[:], T.acc[:, 0:NC], 0.0, None, A.max, None, ["acc"], ["pm"], ["acc"])
        n2, p2 = PK[t + 1]
        mm(n2, p2[:, 0:NC], T.bok32[:], T.pm[:], False, True, ["bok32", "pm"], [n2])
        if t == 0:
            mm("acc", T.acc[:, 0:NC], T.id32[:], T.pm[:], True, False, ["id32", "pm"], ["acc"])
        strike(t, 1)
        report(t)

    pick(2)
    strike(2, 0)
    strike(2, 1)
    before("y", ["sp"], [])
    g.sync.dma_start(T.left[:], T.sp[:]).then_inc(S.stl, 16)
    report(2)
    before("s", ["win0", "win1", "win2", "score0", "score1", "score2"], [])
    act.dma_start(T.win[:], T.res[0:128:16, 0:3]).then_inc(S.sto, 16)
    act.dma_start(T.score[:], T.res[0:128:16, 4:7]).then_inc(S.sto, 16)

    for e in "vspg":
        wait("g", ("c" + e, cnt[e]))
    g.wait_ge(S.sent, sent)
    g.wait_ge(S.sto, 32)
    g.wait_ge(S.stl, 16)
